import numpy as np, ml_dtypes
CORES = [120,124,248,252,376,380,504,508]
N = 8
T, CAP, KR = 256, 48, 256
def entries(a): return a.T.reshape(-1)
def pack(v, P): return np.ascontiguousarray(np.asarray(v, np.int32).reshape(-1, P).T)
def lists(rng, how):
    D = np.stack([rng.permutation(np.repeat(np.arange(N), CAP))[:T] for r in range(N)])
    if how == "full": D = np.stack([(lambda q: rng.permutation(np.concatenate([np.repeat(q[:T // CAP], CAP), np.repeat(q[T // CAP:T // CAP + 1], T % CAP)])))(rng.permutation(N)) for r in range(N)])
    if how == "sorted": D = np.sort(D, axis=1)
    if how == "none": z = int(rng.integers(N)); D = np.stack([rng.permutation(np.repeat(np.delete(np.arange(N), z), CAP))[:T] for r in range(N)]) if CAP * (N - 1) >= T else D
    K_ = KR * D + (np.where(rng.random((N, T)) < 0.5, 0, KR - 1) if how == "edge" else rng.integers(0, KR, (N, T)))
    return {"key": np.stack([pack(K_[r], 16) for r in range(N)])}
def setup_inputs(rng):
    return dict({"x": rng.standard_normal((N, 128, T), dtype=np.float32).astype(ml_dtypes.bfloat16)}, **lists(rng, "uniform"))
def setup_inputs_edge(rng):
    d = setup_inputs(rng); d.update(lists(rng, "edge"))
    for k in ("x",): d[k] = (d[k].astype(np.float32) * 1048576.0).astype(d[k].dtype)
    return d
def setup_inputs_full(rng):
    d = setup_inputs(rng); d.update(lists(rng, "full"))
    for k in ("x",): d[k] = (d[k].astype(np.float32) * (1 / 1024.0)).astype(d[k].dtype)
    return d
def setup_inputs_none(rng):
    d = setup_inputs(rng); d.update(lists(rng, "none"))
    return d
def setup_inputs_sorted(rng):
    d = setup_inputs(rng); d.update(lists(rng, "sorted"))
    return d
def check_inputs(x):
    bad = []
    if x["key"].min() < 0 or x["key"].max() >= N * KR: bad.append("key out of range")
    if max(int(np.bincount(entries(a) // KR, minlength=N).max()) for a in x["key"]) > CAP: bad.append("more than CAP columns of a rank go to one rank")
    return bad
def reference(x, key):
    y = np.zeros((N, 128, N * CAP), x.dtype)
    for r in range(N):
        D = entries(key[r]) // KR
        for d in range(N):
            got = x[r][:, D == d]; y[d][:, CAP * r:CAP * r + got.shape[1]] = got
    return {"y": y}

@@ -1,0 +1,203 @@
+from concourse.bass import DstId, RemoteDMATransfer
+from concourse.mybir import AluOpType
+
+CAP, NR, TC = 48, 8, 256
+W = NR * CAP
+
+SCRATCH = {
+    "xs": ("sbuf", [128, TC], "bfloat16"),
+    "ks": ("sbuf", [128, 16], "int32"),
+    "d16": ("sbuf", [128, 16], "int32"),
+    "qi": ("sbuf", [128, 2], "int32"),
+    "qf": ("sbuf", [128, 4], "float32"),
+    "mi": ("sbuf", [128, 128], "bfloat16"),
+    "pm": ("sbuf", [128, 128], "bfloat16"),
+    "stq": ("sbuf", [128, 128], "bfloat16"),
+    "sts": ("sbuf", [128, 128], "bfloat16"),
+    "ste": ("sbuf", [128, 128], "bfloat16"),
+    "wc": ("sbuf", [128, 128], "bfloat16"),
+    "wp": ("sbuf", [128, 128], "bfloat16"),
+    "w3": ("sbuf", [128, 128], "bfloat16"),
+    "ep": ("sbuf", [128, 17], "bfloat16"),
+    "de": ("sbuf", [128, 16], "bfloat16"),
+    "e48": ("sbuf", [128, 16], "bfloat16"),
+    "oo": ("sbuf", [128, 16], "float32"),
+    "vb": ("sbuf", [128, 16], "bfloat16"),
+    "off": ("sbuf", [128, 16], "uint16"),
+    "pk": ("sbuf", [128, W], "bfloat16"),
+    "land": ("sbuf", [128, W], "bfloat16"),
+    "hop": ("sbuf", [128, 2 * CAP], "bfloat16"),
+    "dps": ("psum", [128, 512], "float32"),
+    "sps": ("psum", [128, 512], "float32"),
+}
+SEMAPHORES = ["kload", "xload", "s_q", "s_mi", "s_pm", "s_p", "s_e0", "s_c1", "s_c2", "s_c3", "s_st", "s_w", "s_w3",
+              "s_d", "s_e", "s_e48", "s_de", "s_mm1", "s_o", "s_v", "s_mm2", "s_off", "s_sc",
+              "hop_in", "near_in", "far_in", "sent", "stored"]
+
+
+def _engines(mask):
+    return [i for i in range(16) if (mask >> i) & 1]
+
+
+def _bits(es):
+    m = 0
+    for e in es:
+        m |= 1 << e
+    return m
+
+
+def _far(c, cores, topo):
+    return [d for d in cores if d != c and not topo.may_write(c, d)]
+
+
+def _relay(c, cores, topo):
+    far = _far(c, cores, topo)
+    for m in cores:
+        if m != c and topo.same_plane(c, m) and topo.die(m) == topo.die(c) and all(topo.may_write(m, f) for f in far):
+            return m
+    return None
+
+
+def _runs(ranks):
+    out = []
+    for r in sorted(ranks):
+        if out and out[-1][0] + out[-1][1] == r:
+            out[-1][1] += 1
+        else:
+            out.append([r, 1])
+    return out
+
+
+def rank_program(g, core, T, topo):
+    rank = T.rank_of(core)
+    if rank is None:
+        return
+    S, A = T.sem, AluOpType
+    v, te = g.vector, g.tensor
+    cores = list(T.cores)
+
+    far = _far(core, cores, topo)
+    near = [d for d in cores if d != core and topo.may_write(core, d)]
+    home = [d for d in near if (topo.host(d), topo.chip(d)) == (topo.host(core), topo.chip(core))]
+    away = [d for d in near if d not in home]
+    plane = [d for d in away if topo.same_plane(core, d)]
+    cable = [d for d in away if d not in plane]
+    order = []
+    for i in range(max(len(plane), len(cable))):
+        order += plane[i:i + 1] + cable[i:i + 1]
+    relay = _relay(core, cores, topo)
+    feeders = [s for s in cores if s != core and _relay(s, cores, topo) == core]
+    off_eng = _engines(topo.mask(core, away[0]))
+    chip_eng = [e for e in _engines(topo.mask(core, home[0])) if e not in off_eng]
+
+    for j in range(8):
+        q = g.sync if j % 2 == 0 else g.scalar
+        q.dma_start(T.ks[16 * j:16 * j + 16, :], T.key[:, :]).then_inc(S.kload, 16)
+    g.sync.dma_start(T.xs[:, :], T.x[:, :]).then_inc(S.xload, 16)
+
+    g.iota(T.qi[:, 0:1], [[0, 1]], 0, 1).then_inc(S.s_q, 1)
+    g.iota(T.mi[:, :], [[1, 128]], 0, 0, allow_small_or_imprecise_dtypes=True).then_inc(S.s_mi, 1)
+    g.iota(T.pm[:, :], [[0, 8], [1, 16]], 0, 0, allow_small_or_imprecise_dtypes=True).then_inc(S.s_pm, 1)
+
+    v.memset(T.ep[:, 0:1], 0.0).then_inc(S.s_e0, 1)
+    v.wait_ge(S.s_q, 1)
+    v.tensor_scalar(T.qi[:, 1:2], T.qi[:, 0:1], 112, None, A.bitwise_and).then_inc(S.s_c1, 1)
+    v.wait_ge(S.s_c1, 1)
+    v.tensor_copy(T.qf[:, 0:2], T.qi[:, 0:2]).then_inc(S.s_c2, 1)
+    v.wait_ge(S.s_c2, 1)
+    qF, sF, eF, s3F = T.qf[:, 0:1], T.qf[:, 1:2], T.qf[:, 2:3], T.qf[:, 3:4]
+    v.tensor_scalar(eF, sF, 16.0, None, A.add).then_inc(S.s_c3, 1)
+    v.tensor_scalar(s3F, sF, 3.0, None, A.mult).then_inc(S.s_c3, 1)
+    v.wait_ge(S.s_mi, 1)
+    v.tensor_scalar(T.stq[:, :], T.mi[:, :], qF, 1.0 / 64, A.is_gt, A.mult).then_inc(S.s_st, 1)
+    v.tensor_scalar(T.sts[:, :], T.mi[:, :], sF, 1.0 / 64, A.is_ge, A.mult).then_inc(S.s_st, 1)
+    v.wait_ge(S.s_c3, 2)
+    v.tensor_scalar(T.ste[:, :], T.mi[:, :], eF, 1.0 / 64, A.is_ge, A.mult).then_inc(S.s_st, 1)
+    v.wait_ge(S.s_st, 3)
+    v.tensor_tensor(T.wc[:, :], T.stq[:, :], T.ste[:, :], A.subtract).then_inc(S.s_w, 1)
+    v.tensor_tensor(T.wp[:, :], T.sts[:, :], T.stq[:, :], A.subtract).then_inc(S.s_w, 1)
+    v.wait_ge(S.s_pm, 1)
+    v.tensor_scalar(T.w3[:, :], T.pm[:, :], sF, qF, A.add, A.is_equal).then_inc(S.s_w3, 1)
+    v.memset(T.pk[:, :], 0.0).then_inc(S.s_p, 1)
+
+    cur, prev = T.ep[:, 1:17], T.ep[:, 0:16]
+    v.wait_ge(S.kload, 128)
+    v.tensor_scalar(T.d16[:, :], T.ks[:, :], 4, 112, A.arith_shift_right, A.bitwise_and).then_inc(S.s_d, 1)
+    v.wait_ge(S.s_d, 1)
+    v.tensor_scalar(cur, T.d16[:, :], sF, 64.0, A.is_equal, A.mult).then_inc(S.s_e, 1)
+    v.tensor_scalar(T.e48[:, :], T.d16[:, :], sF, s3F, A.is_equal, A.mult).then_inc(S.s_e48, 1)
+    v.wait_ge(S.s_e, 1)
+    v.wait_ge(S.s_e0, 1)
+    v.tensor_tensor(T.de[:, :], cur, prev, A.subtract).then_inc(S.s_de, 1)
+
+    te.wait_ge(S.s_w, 2)
+    te.wait_ge(S.s_e0, 1)
+    te.wait_ge(S.s_e, 1)
+    te.matmul(T.dps[:, 0:16], T.wc[:, :], cur, True, False)
+    te.matmul(T.dps[:, 0:16], T.wp[:, :], prev, False, True).then_inc(S.s_mm1, 1)
+    te.wait_ge(S.s_w3, 1)
+    te.wait_ge(S.s_e48, 1)
+    te.matmul(T.sps[:, 0:16], T.w3[:, :], T.e48[:, :], True, False)
+
+    v.wait_ge(S.s_de, 1)
+    v.wait_ge(S.s_mm1, 1)
+    v.tensor_tensor_scan(T.oo[:, :], T.dps[:, 0:16], T.de[:, :], -64.0, A.add, A.add).then_inc(S.s_o, 1)
+    v.wait_ge(S.s_o, 1)
+    v.tensor_scalar(T.vb[:, :], T.oo[:, :], 0.0, None, A.max).then_inc(S.s_v, 1)
+    te.wait_ge(S.s_v, 1)
+    te.matmul(T.sps[:, 0:16], T.w3[:, :], T.vb[:, :], False, True).then_inc(S.s_mm2, 1)
+    v.wait_ge(S.s_mm2, 1)
+    v.tensor_copy(T.off[:, :], T.sps[:, 0:16]).then_inc(S.s_off, 1)
+
+    v.wait_ge(S.s_off, 1)
+    v.wait_ge(S.s_p, 1)
+    v.wait_ge(S.xload, 16)
+    v.tensor_copy(T.pk[:, 0:W].indirect(T.off[:, 0:16]), T.xs[:, 0:TC]).then_inc(S.s_sc, 1)
+
+    def blk(buf, r, n=1):
+        return buf[:, CAP * r:CAP * (r + n)]
+
+    sent = 0
+    g.wait_ge(S.s_sc, 1)
+    fr = sorted(T.rank_of(d) for d in far)
+    rid, pid = topo.addr(relay, core)
+    g.remote_dma(T.hop[:, :], blk(T.pk, fr[0], len(fr)), S.hop_in, S.sent, pid, rid, _bits(off_eng))
+    sent += len(off_eng)
+    per = len(off_eng) // len(order)
+    trs = []
+    for i, d in enumerate(order):
+        rid, pid = topo.addr(d, core)
+        trs.append(RemoteDMATransfer(dst_ids=[DstId(rid=rid, pnc=pid)], dma_engine_mask=_bits(off_eng[i::len(order)]),
+                                     remote_sem=S.near_in, src=blk(T.pk, T.rank_of(d)), dst=blk(T.land, rank)))
+        sent += per
+    g.remote_dma_fused(trs, local_sem=S.sent)
+    rid, pid = topo.addr(home[0], core)
+    g.remote_dma(blk(T.land, rank), blk(T.pk, T.rank_of(home[0])), S.near_in, S.sent, pid, rid, _bits(chip_eng))
+    sent += len(chip_eng)
+
+    feeder = feeders[0]
+    g.wait_ge(S.hop_in, len(off_eng))
+    dsts = sorted(_far(feeder, cores, topo), key=T.rank_of)
+    half = len(off_eng) // len(dsts)
+    trs = []
+    for i, d in enumerate(dsts):
+        rid, pid = topo.addr(d, core)
+        trs.append(RemoteDMATransfer(dst_ids=[DstId(rid=rid, pnc=pid)], dma_engine_mask=_bits(off_eng[i::len(dsts)]),
+                                     remote_sem=S.far_in, src=blk(T.hop, i), dst=blk(T.land, T.rank_of(feeder))))
+        sent += half
+    g.remote_dma_fused(trs, local_sem=S.sent)
+
+    stored = 0
+    g.scalar.wait_ge(S.s_sc, 1)
+    g.scalar.dma_start(blk(T.y, rank), blk(T.pk, rank)).then_inc(S.stored, 16)
+    stored += 16
+    g.scalar.wait_ge(S.near_in, per * len(order) + len(chip_eng))
+    for r0, n in _runs(T.rank_of(d) for d in near):
+        g.scalar.dma_start(blk(T.y, r0, n), blk(T.land, r0, n)).then_inc(S.stored, 16)
+        stored += 16
+    g.sync.wait_ge(S.far_in, half * len(far))
+    for r0, n in _runs(fr):
+        g.sync.dma_start(blk(T.y, r0, n), blk(T.land, r0, n)).then_inc(S.stored, 16)
+        stored += 16
+    g.wait_ge(S.sent, sent)
+    g.wait_ge(S.stored, stored)

@@ -6,6 +6,7 @@ W = NR * CAP
 
 SCRATCH = {
     "xs": ("sbuf", [128, TC], "bfloat16"),
+    "x2": ("sbuf", [128, TC], "bfloat16"),
     "ks": ("sbuf", [128, 16], "int32"),
     "d16": ("sbuf", [128, 16], "int32"),
     "qi": ("sbuf", [128, 2], "int32"),
@@ -24,15 +25,17 @@ SCRATCH = {
     "oo": ("sbuf", [128, 16], "float32"),
     "vb": ("sbuf", [128, 16], "bfloat16"),
     "off": ("sbuf", [128, 16], "uint16"),
+    "off2": ("sbuf", [128, 16], "uint16"),
     "pk": ("sbuf", [128, W], "bfloat16"),
+    "pk2": ("sbuf", [128, W], "bfloat16"),
     "land": ("sbuf", [128, W], "bfloat16"),
     "hop": ("sbuf", [128, 2 * CAP], "bfloat16"),
     "dps": ("psum", [128, 512], "float32"),
     "sps": ("psum", [128, 512], "float32"),
 }
-SEMAPHORES = ["kload", "xload", "s_q", "s_mi", "s_pm", "s_p", "s_e0", "s_c1", "s_c2", "s_c3", "s_st", "s_w", "s_w3",
-              "s_d", "s_e", "s_e48", "s_de", "s_mm1", "s_o", "s_v", "s_mm2", "s_off", "s_sc",
-              "hop_in", "near_in", "far_in", "sent", "stored"]
+SEMAPHORES = ["kload", "xload", "s_q", "s_mi", "s_pm", "s_p", "s_p2", "s_e0", "s_c1", "s_c2", "s_c3", "s_st", "s_w", "s_w3",
+              "s_d", "s_e", "s_e48", "s_de", "s_mm1", "s_o", "s_v", "s_mm2", "s_off", "s_sc", "s_sc2",
+              "x2_in", "off2_in", "hop_in", "near_in", "far_in", "sent", "stored"]
 
 
 def _engines(mask):
@@ -76,9 +79,13 @@ def rank_program(g, core, T, topo):
     v, te = g.vector, g.tensor
     cores = list(T.cores)
 
+    def blk(buf, r, n=1):
+        return buf[:, CAP * r:CAP * (r + n)]
+
     far = _far(core, cores, topo)
     near = [d for d in cores if d != core and topo.may_write(core, d)]
     home = [d for d in near if (topo.host(d), topo.chip(d)) == (topo.host(core), topo.chip(core))]
+    mate = home[0]
     away = [d for d in near if d not in home]
     plane = [d for d in away if topo.same_plane(core, d)]
     cable = [d for d in away if d not in plane]
@@ -86,9 +93,11 @@ def rank_program(g, core, T, topo):
     for i in range(max(len(plane), len(cable))):
         order += plane[i:i + 1] + cable[i:i + 1]
     relay = _relay(core, cores, topo)
-    feeders = [s for s in cores if s != core and _relay(s, cores, topo) == core]
+    feeder = [s for s in cores if s != core and _relay(s, cores, topo) == core][0]
+    all_eng = _engines(topo.mask(core, mate))
     off_eng = _engines(topo.mask(core, away[0]))
-    chip_eng = [e for e in _engines(topo.mask(core, home[0])) if e not in off_eng]
+    chip_eng = [e for e in all_eng if e not in off_eng]
+    mrid, mpid = topo.addr(mate, core)
 
     for j in range(8):
         q = g.sync if j % 2 == 0 else g.scalar
@@ -98,6 +107,11 @@ def rank_program(g, core, T, topo):
     g.iota(T.qi[:, 0:1], [[0, 1]], 0, 1).then_inc(S.s_q, 1)
     g.iota(T.mi[:, :], [[1, 128]], 0, 0, allow_small_or_imprecise_dtypes=True).then_inc(S.s_mi, 1)
     g.iota(T.pm[:, :], [[0, 8], [1, 16]], 0, 0, allow_small_or_imprecise_dtypes=True).then_inc(S.s_pm, 1)
+
+    sent = 0
+    g.wait_ge(S.xload, 16)
+    g.remote_dma(T.x2[:, :], T.xs[:, :], S.x2_in, S.sent, mpid, mrid, _bits(all_eng))
+    sent += len(all_eng)
 
     v.memset(T.ep[:, 0:1], 0.0).then_inc(S.s_e0, 1)
     v.wait_ge(S.s_q, 1)
@@ -119,6 +133,7 @@ def rank_program(g, core, T, topo):
     v.wait_ge(S.s_pm, 1)
     v.tensor_scalar(T.w3[:, :], T.pm[:, :], sF, qF, A.add, A.is_equal).then_inc(S.s_w3, 1)
     v.memset(T.pk[:, :], 0.0).then_inc(S.s_p, 1)
+    v.memset(blk(T.pk2, rank), 0.0).then_inc(S.s_p2, 1)
 
     cur, prev = T.ep[:, 1:17], T.ep[:, 0:16]
     v.wait_ge(S.kload, 128)
@@ -154,10 +169,11 @@ def rank_program(g, core, T, topo):
     v.wait_ge(S.xload, 16)
     v.tensor_copy(T.pk[:, 0:W].indirect(T.off[:, 0:16]), T.xs[:, 0:TC]).then_inc(S.s_sc, 1)
 
-    def blk(buf, r, n=1):
-        return buf[:, CAP * r:CAP * (r + n)]
+    v.wait_ge(S.s_p2, 1)
+    v.wait_ge(S.x2_in, len(all_eng))
+    v.wait_ge(S.off2_in, len(chip_eng))
+    v.tensor_copy(T.pk2[:, 0:W].indirect(T.off2[:, 0:16]), T.x2[:, 0:TC]).then_inc(S.s_sc2, 1)
 
-    sent = 0
     g.wait_ge(S.s_sc, 1)
     fr = sorted(T.rank_of(d) for d in far)
     rid, pid = topo.addr(relay, core)
@@ -171,11 +187,9 @@ def rank_program(g, core, T, topo):
                                      remote_sem=S.near_in, src=blk(T.pk, T.rank_of(d)), dst=blk(T.land, rank)))
         sent += per
     g.remote_dma_fused(trs, local_sem=S.sent)
-    rid, pid = topo.addr(home[0], core)
-    g.remote_dma(blk(T.land, rank), blk(T.pk, T.rank_of(home[0])), S.near_in, S.sent, pid, rid, _bits(chip_eng))
+    g.remote_dma(T.off2[:, :], T.off[:, :], S.off2_in, S.sent, mpid, mrid, _bits(chip_eng))
     sent += len(chip_eng)
 
-    feeder = feeders[0]
     g.wait_ge(S.hop_in, len(off_eng))
     dsts = sorted(_far(feeder, cores, topo), key=T.rank_of)
     half = len(off_eng) // len(dsts)
@@ -191,10 +205,13 @@ def rank_program(g, core, T, topo):
     g.scalar.wait_ge(S.s_sc, 1)
     g.scalar.dma_start(blk(T.y, rank), blk(T.pk, rank)).then_inc(S.stored, 16)
     stored += 16
-    g.scalar.wait_ge(S.near_in, per * len(order) + len(chip_eng))
-    for r0, n in _runs(T.rank_of(d) for d in near):
+    g.scalar.wait_ge(S.near_in, per * len(order))
+    for r0, n in _runs(T.rank_of(d) for d in away):
         g.scalar.dma_start(blk(T.y, r0, n), blk(T.land, r0, n)).then_inc(S.stored, 16)
         stored += 16
+    g.sync.wait_ge(S.s_sc2, 1)
+    g.sync.dma_start(blk(T.y, T.rank_of(mate)), blk(T.pk2, rank)).then_inc(S.stored, 16)
+    stored += 16
     g.sync.wait_ge(S.far_in, half * len(far))
     for r0, n in _runs(fr):
         g.sync.dma_start(blk(T.y, r0, n), blk(T.land, r0, n)).then_inc(S.stored, 16)

@@ -1,5 +1,5 @@
 from concourse.bass import DstId, RemoteDMATransfer
-from concourse.mybir import AluOpType
+from concourse.mybir import AluOpType, ActivationFunctionType
 
 CAP, NR, TC = 48, 8, 256
 W = NR * CAP
@@ -8,20 +8,23 @@ SCRATCH = {
     "xs": ("sbuf", [128, TC], "bfloat16"),
     "x2": ("sbuf", [128, TC], "bfloat16"),
     "ks": ("sbuf", [128, 16], "int32"),
-    "d16": ("sbuf", [128, 16], "int32"),
-    "qi": ("sbuf", [128, 2], "int32"),
+    "qi": ("sbuf", [128, 1], "int32"),
+    "qa": ("sbuf", [128, 3], "int32"),
     "qf": ("sbuf", [128, 4], "float32"),
-    "mi": ("sbuf", [128, 128], "bfloat16"),
+    "um": ("sbuf", [128, 136], "bfloat16"),
     "pm": ("sbuf", [128, 128], "bfloat16"),
-    "stq": ("sbuf", [128, 128], "bfloat16"),
-    "sts": ("sbuf", [128, 128], "bfloat16"),
-    "ste": ("sbuf", [128, 128], "bfloat16"),
+    "a1": ("sbuf", [128, 128], "bfloat16"),
+    "a2": ("sbuf", [128, 128], "bfloat16"),
+    "b1": ("sbuf", [128, 128], "bfloat16"),
+    "b2": ("sbuf", [128, 128], "bfloat16"),
     "wc": ("sbuf", [128, 128], "bfloat16"),
     "wp": ("sbuf", [128, 128], "bfloat16"),
+    "j0": ("sbuf", [128, 128], "bfloat16"),
+    "j16": ("sbuf", [128, 128], "bfloat16"),
     "w3": ("sbuf", [128, 128], "bfloat16"),
+    "w48": ("sbuf", [128, 128], "bfloat16"),
     "ep": ("sbuf", [128, 17], "bfloat16"),
-    "de": ("sbuf", [128, 16], "bfloat16"),
-    "e48": ("sbuf", [128, 16], "bfloat16"),
+    "zz": ("sbuf", [128, 16], "float32"),
     "oo": ("sbuf", [128, 16], "float32"),
     "vb": ("sbuf", [128, 16], "bfloat16"),
     "off": ("sbuf", [128, 16], "uint16"),
@@ -31,10 +34,11 @@ SCRATCH = {
     "land": ("sbuf", [128, W], "bfloat16"),
     "hop": ("sbuf", [128, 2 * CAP], "bfloat16"),
     "dps": ("psum", [128, 512], "float32"),
+    "eps": ("psum", [128, 512], "float32"),
     "sps": ("psum", [128, 512], "float32"),
 }
-SEMAPHORES = ["kload", "xload", "s_q", "s_mi", "s_pm", "s_p", "s_p2", "s_e0", "s_c1", "s_c2", "s_c3", "s_st", "s_w", "s_w3",
-              "s_d", "s_e", "s_e48", "s_de", "s_mm1", "s_o", "s_v", "s_mm2", "s_off", "s_sc", "s_sc2",
+SEMAPHORES = ["kload", "xload", "s_q", "s_u", "s_pm", "s_p", "s_p2", "s_e0", "s_c1", "s_pf", "s_c2", "s_a1", "s_a2", "s_b1",
+              "s_b2", "s_w", "s_j", "s_w3", "s_e", "s_mm1", "s_eps", "s_o", "s_v", "s_mm2", "s_off", "s_sc", "s_sc2",
               "x2_in", "off2_in", "hop_in", "near_in", "far_in", "sent", "stored"]
 
 
@@ -75,8 +79,8 @@ def rank_program(g, core, T, topo):
     rank = T.rank_of(core)
     if rank is None:
         return
-    S, A = T.sem, AluOpType
-    v, te = g.vector, g.tensor
+    S, A, F = T.sem, AluOpType, ActivationFunctionType
+    v, te, sc = g.vector, g.tensor, g.scalar
     cores = list(T.cores)
 
     def blk(buf, r, n=1):
@@ -105,7 +109,7 @@ def rank_program(g, core, T, topo):
     g.sync.dma_start(T.xs[:, :], T.x[:, :]).then_inc(S.xload, 16)
 
     g.iota(T.qi[:, 0:1], [[0, 1]], 0, 1).then_inc(S.s_q, 1)
-    g.iota(T.mi[:, :], [[1, 128]], 0, 0, allow_small_or_imprecise_dtypes=True).then_inc(S.s_mi, 1)
+    g.iota(T.um[:, :], [[2, 136]], 0, -2, allow_small_or_imprecise_dtypes=True).then_inc(S.s_u, 1)
     g.iota(T.pm[:, :], [[0, 8], [1, 16]], 0, 0, allow_small_or_imprecise_dtypes=True).then_inc(S.s_pm, 1)
 
     sent = 0
@@ -113,59 +117,75 @@ def rank_program(g, core, T, topo):
     g.remote_dma(T.x2[:, :], T.xs[:, :], S.x2_in, S.sent, mpid, mrid, _bits(all_eng))
     sent += len(all_eng)
 
-    v.memset(T.ep[:, 0:1], 0.0).then_inc(S.s_e0, 1)
+    pI, sI, bI = T.qa[:, 0:1], T.qa[:, 1:2], T.qa[:, 2:3]
+    pF, lowF, sgnF, s48 = [T.qf[:, i:i + 1] for i in range(4)]
+    u0 = T.um[:, 0:128]
     v.wait_ge(S.s_q, 1)
-    v.tensor_scalar(T.qi[:, 1:2], T.qi[:, 0:1], 112, None, A.bitwise_and).then_inc(S.s_c1, 1)
-    v.wait_ge(S.s_c1, 1)
-    v.tensor_copy(T.qf[:, 0:2], T.qi[:, 0:2]).then_inc(S.s_c2, 1)
-    v.wait_ge(S.s_c2, 1)
-    qF, sF, eF, s3F = T.qf[:, 0:1], T.qf[:, 1:2], T.qf[:, 2:3], T.qf[:, 3:4]
-    v.tensor_scalar(eF, sF, 16.0, None, A.add).then_inc(S.s_c3, 1)
-    v.tensor_scalar(s3F, sF, 3.0, None, A.mult).then_inc(S.s_c3, 1)
-    v.wait_ge(S.s_mi, 1)
-    v.tensor_scalar(T.stq[:, :], T.mi[:, :], qF, 1.0 / 64, A.is_gt, A.mult).then_inc(S.s_st, 1)
-    v.tensor_scalar(T.sts[:, :], T.mi[:, :], sF, 1.0 / 64, A.is_ge, A.mult).then_inc(S.s_st, 1)
-    v.wait_ge(S.s_c3, 2)
-    v.tensor_scalar(T.ste[:, :], T.mi[:, :], eF, 1.0 / 64, A.is_ge, A.mult).then_inc(S.s_st, 1)
-    v.wait_ge(S.s_st, 3)
-    v.tensor_tensor(T.wc[:, :], T.stq[:, :], T.ste[:, :], A.subtract).then_inc(S.s_w, 1)
-    v.tensor_tensor(T.wp[:, :], T.sts[:, :], T.stq[:, :], A.subtract).then_inc(S.s_w, 1)
+    v.tensor_scalar(pI, T.qi[:, 0:1], 15, None, A.bitwise_and).then_inc(S.s_c1, 1)
+    v.tensor_scalar(sI, T.qi[:, 0:1], 112, None, A.bitwise_and).then_inc(S.s_c1, 1)
+    v.tensor_scalar(bI, T.qi[:, 0:1], 16, None, A.bitwise_and).then_inc(S.s_c1, 1)
+    v.wait_ge(S.s_c1, 3)
+    v.tensor_copy(pF, pI).then_inc(S.s_pf, 1)
+    v.tensor_scalar(lowF, sI, 16.0, None, A.mult).then_inc(S.s_c2, 1)
+    v.tensor_scalar(sgnF, bI, -0.125, 1.0, A.mult, A.add).then_inc(S.s_c2, 1)
+    v.tensor_scalar(s48, bI, -6.0, 48.0, A.mult, A.add).then_inc(S.s_c2, 1)
+    v.memset(T.ep[:, 0:1], 0.0).then_inc(S.s_e0, 1)
+    v.memset(T.zz[:, :], 0.0).then_inc(S.s_e0, 1)
+
+    sc.wait_ge(S.s_u, 1)
+    sc.wait_ge(S.s_pf, 1)
+    sc.activation(T.a1[:, :], u0, F.Abs, bias=pF, scale=1.0).then_inc(S.s_a1, 1)
+    sc.activation(T.a2[:, :], T.um[:, 8:136], F.Abs, bias=pF, scale=1.0).then_inc(S.s_a2, 1)
+    sc.wait_ge(S.s_a1, 1)
+    sc.activation(T.b1[:, :], T.a1[:, :], F.Abs, bias=-16.0, scale=1.0).then_inc(S.s_b1, 1)
+    sc.wait_ge(S.s_a2, 1)
+    sc.activation(T.b2[:, :], T.a2[:, :], F.Abs, bias=-16.0, scale=1.0).then_inc(S.s_b2, 1)
+    sc.wait_ge(S.s_pm, 1)
+    for j in range(W // 128):
+        sc.activation(T.pk[:, 128 * j:128 * j + 128], T.pm[:, :], F.Copy, scale=0.0).then_inc(S.s_p, 1)
+    sc.activation(blk(T.pk2, rank), T.pm[:, 0:CAP], F.Copy, scale=0.0).then_inc(S.s_p2, 1)
+
+    v.wait_ge(S.s_u, 1)
+    v.tensor_scalar(T.j0[:, :], u0, 0.0, None, A.is_equal).then_inc(S.s_j, 1)
+    v.tensor_scalar(T.j16[:, :], u0, -32.0, None, A.is_equal).then_inc(S.s_j, 1)
+    v.wait_ge(S.s_pf, 1)
+    v.wait_ge(S.s_c2, 3)
     v.wait_ge(S.s_pm, 1)
-    v.tensor_scalar(T.w3[:, :], T.pm[:, :], sF, qF, A.add, A.is_equal).then_inc(S.s_w3, 1)
-    v.memset(T.pk[:, :], 0.0).then_inc(S.s_p, 1)
-    v.memset(blk(T.pk2, rank), 0.0).then_inc(S.s_p2, 1)
+    v.tensor_scalar(T.w48[:, :], T.pm[:, :], pF, s48, A.is_equal, A.mult).then_inc(S.s_w3, 1)
+    v.tensor_scalar(T.w3[:, :], T.pm[:, :], pF, None, A.is_equal).then_inc(S.s_w3, 1)
+    v.wait_ge(S.s_b1, 1)
+    v.tensor_scalar(T.wc[:, :], T.b1[:, :], pF, 16.0, A.add, A.is_lt).then_inc(S.s_w, 1)
+    v.wait_ge(S.s_b2, 1)
+    v.tensor_scalar(T.wp[:, :], T.b2[:, :], pF, None, A.is_le).then_inc(S.s_w, 1)
 
     cur, prev = T.ep[:, 1:17], T.ep[:, 0:16]
     v.wait_ge(S.kload, 128)
-    v.tensor_scalar(T.d16[:, :], T.ks[:, :], 4, 112, A.arith_shift_right, A.bitwise_and).then_inc(S.s_d, 1)
-    v.wait_ge(S.s_d, 1)
-    v.tensor_scalar(cur, T.d16[:, :], sF, 64.0, A.is_equal, A.mult).then_inc(S.s_e, 1)
-    v.tensor_scalar(T.e48[:, :], T.d16[:, :], sF, s3F, A.is_equal, A.mult).then_inc(S.s_e48, 1)
-    v.wait_ge(S.s_e, 1)
-    v.wait_ge(S.s_e0, 1)
-    v.tensor_tensor(T.de[:, :], cur, prev, A.subtract).then_inc(S.s_de, 1)
+    v.tensor_scalar(cur, T.ks[:, :], lowF, sgnF, A.is_ge, A.mult).then_inc(S.s_e, 1)
 
     te.wait_ge(S.s_w, 2)
-    te.wait_ge(S.s_e0, 1)
+    te.wait_ge(S.s_e0, 2)
     te.wait_ge(S.s_e, 1)
     te.matmul(T.dps[:, 0:16], T.wc[:, :], cur, True, False)
     te.matmul(T.dps[:, 0:16], T.wp[:, :], prev, False, True).then_inc(S.s_mm1, 1)
-    te.wait_ge(S.s_w3, 1)
-    te.wait_ge(S.s_e48, 1)
-    te.matmul(T.sps[:, 0:16], T.w3[:, :], T.e48[:, :], True, False)
+    te.wait_ge(S.s_j, 2)
+    te.matmul(T.eps[:, 0:16], T.j0[:, :], cur, True, False)
+    te.matmul(T.eps[:, 0:16], T.j16[:, :], cur, False, True).then_inc(S.s_eps, 1)
+    te.wait_ge(S.s_w3, 2)
+    te.matmul(T.sps[:, 0:16], T.w48[:, :], cur, True, False)
 
-    v.wait_ge(S.s_de, 1)
+    v.wait_ge(S.s_e0, 2)
     v.wait_ge(S.s_mm1, 1)
-    v.tensor_tensor_scan(T.oo[:, :], T.dps[:, 0:16], T.de[:, :], -64.0, A.add, A.add).then_inc(S.s_o, 1)
+    v.tensor_tensor_scan(T.oo[:, :], T.dps[:, 0:16], T.zz[:, :], 0.0, A.add, A.add).then_inc(S.s_o, 1)
     v.wait_ge(S.s_o, 1)
-    v.tensor_scalar(T.vb[:, :], T.oo[:, :], 0.0, None, A.max).then_inc(S.s_v, 1)
+    v.wait_ge(S.s_eps, 1)
+    v.tensor_tensor(T.vb[:, :], T.oo[:, :], T.eps[:, 0:16], A.mult).then_inc(S.s_v, 1)
     te.wait_ge(S.s_v, 1)
     te.matmul(T.sps[:, 0:16], T.w3[:, :], T.vb[:, :], False, True).then_inc(S.s_mm2, 1)
     v.wait_ge(S.s_mm2, 1)
-    v.tensor_copy(T.off[:, :], T.sps[:, 0:16]).then_inc(S.s_off, 1)
+    v.tensor_scalar(T.off[:, :], T.sps[:, 0:16], -48.0, None, A.add).then_inc(S.s_off, 1)
 
     v.wait_ge(S.s_off, 1)
-    v.wait_ge(S.s_p, 1)
+    v.wait_ge(S.s_p, W // 128)
     v.wait_ge(S.xload, 16)
     v.tensor_copy(T.pk[:, 0:W].indirect(T.off[:, 0:16]), T.xs[:, 0:TC]).then_inc(S.s_sc, 1)
 

from concourse.bass import DstId, RemoteDMATransfer
from concourse.mybir import AluOpType, ActivationFunctionType

CAP, NR, TC = 48, 8, 256
W = NR * CAP

SCRATCH = {
    "xs": ("sbuf", [128, TC], "bfloat16"),
    "x2": ("sbuf", [128, TC], "bfloat16"),
    "ks": ("sbuf", [128, 16], "int32"),
    "qi": ("sbuf", [128, 1], "int32"),
    "qa": ("sbuf", [128, 3], "int32"),
    "qf": ("sbuf", [128, 4], "float32"),
    "um": ("sbuf", [128, 136], "bfloat16"),
    "pm": ("sbuf", [128, 128], "bfloat16"),
    "a1": ("sbuf", [128, 128], "bfloat16"),
    "a2": ("sbuf", [128, 128], "bfloat16"),
    "b1": ("sbuf", [128, 128], "bfloat16"),
    "b2": ("sbuf", [128, 128], "bfloat16"),
    "wc": ("sbuf", [128, 128], "bfloat16"),
    "wp": ("sbuf", [128, 128], "bfloat16"),
    "j0": ("sbuf", [128, 128], "bfloat16"),
    "j16": ("sbuf", [128, 128], "bfloat16"),
    "w3": ("sbuf", [128, 128], "bfloat16"),
    "w48": ("sbuf", [128, 128], "bfloat16"),
    "ep": ("sbuf", [128, 17], "bfloat16"),
    "zz": ("sbuf", [128, 16], "float32"),
    "oo": ("sbuf", [128, 16], "float32"),
    "vb": ("sbuf", [128, 16], "bfloat16"),
    "off": ("sbuf", [128, 16], "uint16"),
    "off2": ("sbuf", [128, 16], "uint16"),
    "pk": ("sbuf", [128, W], "bfloat16"),
    "pk2": ("sbuf", [128, W], "bfloat16"),
    "land": ("sbuf", [128, W], "bfloat16"),
    "hop": ("sbuf", [128, 2 * CAP], "bfloat16"),
    "dps": ("psum", [128, 512], "float32"),
    "eps": ("psum", [128, 512], "float32"),
    "sps": ("psum", [128, 512], "float32"),
}
SEMAPHORES = ["kload", "xload", "s_q", "s_u", "s_pm", "s_p", "s_p2", "s_e0", "s_c1", "s_pf", "s_c2", "s_a1", "s_a2", "s_b1",
              "s_b2", "s_w", "s_j", "s_w3", "s_e", "s_mm1", "s_eps", "s_o", "s_v", "s_mm2", "s_off", "s_sc", "s_sc2",
              "x2_in", "off2_in", "hop_in", "near_in", "far_in", "sent", "stored"]


def _engines(mask):
    return [i for i in range(16) if (mask >> i) & 1]


def _bits(es):
    m = 0
    for e in es:
        m |= 1 << e
    return m


def _far(c, cores, topo):
    return [d for d in cores if d != c and not topo.may_write(c, d)]


def _relay(c, cores, topo):
    far = _far(c, cores, topo)
    for m in cores:
        if m != c and topo.same_plane(c, m) and topo.die(m) == topo.die(c) and all(topo.may_write(m, f) for f in far):
            return m
    return None


def _runs(ranks):
    out = []
    for r in sorted(ranks):
        if out and out[-1][0] + out[-1][1] == r:
            out[-1][1] += 1
        else:
            out.append([r, 1])
    return out


def rank_program(g, core, T, topo):
    rank = T.rank_of(core)
    if rank is None:
        return
    S, A, F = T.sem, AluOpType, ActivationFunctionType
    v, te, sc = g.vector, g.tensor, g.scalar
    cores = list(T.cores)

    def blk(buf, r, n=1):
        return buf[:, CAP * r:CAP * (r + n)]

    far = _far(core, cores, topo)
    near = [d for d in cores if d != core and topo.may_write(core, d)]
    home = [d for d in near if (topo.host(d), topo.chip(d)) == (topo.host(core), topo.chip(core))]
    mate = home[0]
    away = [d for d in near if d not in home]
    plane = [d for d in away if topo.same_plane(core, d)]
    cable = [d for d in away if d not in plane]
    order = []
    for i in range(max(len(plane), len(cable))):
        order += plane[i:i + 1] + cable[i:i + 1]
    relay = _relay(core, cores, topo)
    feeder = [s for s in cores if s != core and _relay(s, cores, topo) == core][0]
    all_eng = _engines(topo.mask(core, mate))
    off_eng = _engines(topo.mask(core, away[0]))
    chip_eng = [e for e in all_eng if e not in off_eng]
    mrid, mpid = topo.addr(mate, core)

    for j in range(8):
        q = g.sync if j % 2 == 0 else g.scalar
        q.dma_start(T.ks[16 * j:16 * j + 16, :], T.key[:, :]).then_inc(S.kload, 16)
    g.sync.dma_start(T.xs[:, :], T.x[:, :]).then_inc(S.xload, 16)

    g.iota(T.qi[:, 0:1], [[0, 1]], 0, 1).then_inc(S.s_q, 1)
    g.iota(T.um[:, :], [[2, 136]], 0, -2, allow_small_or_imprecise_dtypes=True).then_inc(S.s_u, 1)
    g.iota(T.pm[:, :], [[0, 8], [1, 16]], 0, 0, allow_small_or_imprecise_dtypes=True).then_inc(S.s_pm, 1)

    sent = 0
    g.wait_ge(S.xload, 16)
    g.remote_dma(T.x2[:, :], T.xs[:, :], S.x2_in, S.sent, mpid, mrid, _bits(all_eng))
    sent += len(all_eng)

    pI, sI, bI = T.qa[:, 0:1], T.qa[:, 1:2], T.qa[:, 2:3]
    pF, lowF, sgnF, s48 = [T.qf[:, i:i + 1] for i in range(4)]
    u0 = T.um[:, 0:128]
    v.wait_ge(S.s_q, 1)
    v.tensor_scalar(pI, T.qi[:, 0:1], 15, None, A.bitwise_and).then_inc(S.s_c1, 1)
    v.tensor_scalar(sI, T.qi[:, 0:1], 112, None, A.bitwise_and).then_inc(S.s_c1, 1)
    v.tensor_scalar(bI, T.qi[:, 0:1], 16, None, A.bitwise_and).then_inc(S.s_c1, 1)
    v.wait_ge(S.s_c1, 3)
    v.tensor_copy(pF, pI).then_inc(S.s_pf, 1)
    v.tensor_scalar(lowF, sI, 16.0, None, A.mult).then_inc(S.s_c2, 1)
    v.tensor_scalar(sgnF, bI, -0.125, 1.0, A.mult, A.add).then_inc(S.s_c2, 1)
    v.tensor_scalar(s48, bI, -6.0, 48.0, A.mult, A.add).then_inc(S.s_c2, 1)
    v.memset(T.ep[:, 0:1], 0.0).then_inc(S.s_e0, 1)
    v.memset(T.zz[:, :], 0.0).then_inc(S.s_e0, 1)

    sc.wait_ge(S.s_u, 1)
    sc.wait_ge(S.s_pf, 1)
    sc.activation(T.a1[:, :], u0, F.Abs, bias=pF, scale=1.0).then_inc(S.s_a1, 1)
    sc.activation(T.a2[:, :], T.um[:, 8:136], F.Abs, bias=pF, scale=1.0).then_inc(S.s_a2, 1)
    sc.wait_ge(S.s_a1, 1)
    sc.activation(T.b1[:, :], T.a1[:, :], F.Abs, bias=-16.0, scale=1.0).then_inc(S.s_b1, 1)
    sc.wait_ge(S.s_a2, 1)
    sc.activation(T.b2[:, :], T.a2[:, :], F.Abs, bias=-16.0, scale=1.0).then_inc(S.s_b2, 1)
    sc.wait_ge(S.s_pm, 1)
    for j in range(W // 128):
        sc.activation(T.pk[:, 128 * j:128 * j + 128], T.pm[:, :], F.Copy, scale=0.0).then_inc(S.s_p, 1)
    sc.activation(blk(T.pk2, rank), T.pm[:, 0:CAP], F.Copy, scale=0.0).then_inc(S.s_p2, 1)

    v.wait_ge(S.s_u, 1)
    v.tensor_scalar(T.j0[:, :], u0, 0.0, None, A.is_equal).then_inc(S.s_j, 1)
    v.tensor_scalar(T.j16[:, :], u0, -32.0, None, A.is_equal).then_inc(S.s_j, 1)
    v.wait_ge(S.s_pf, 1)
    v.wait_ge(S.s_c2, 3)
    v.wait_ge(S.s_pm, 1)
    v.tensor_scalar(T.w48[:, :], T.pm[:, :], pF, s48, A.is_equal, A.mult).then_inc(S.s_w3, 1)
    v.tensor_scalar(T.w3[:, :], T.pm[:, :], pF, None, A.is_equal).then_inc(S.s_w3, 1)
    v.wait_ge(S.s_b1, 1)
    v.tensor_scalar(T.wc[:, :], T.b1[:, :], pF, 16.0, A.add, A.is_lt).then_inc(S.s_w, 1)
    v.wait_ge(S.s_b2, 1)
    v.tensor_scalar(T.wp[:, :], T.b2[:, :], pF, None, A.is_le).then_inc(S.s_w, 1)

    cur, prev = T.ep[:, 1:17], T.ep[:, 0:16]
    v.wait_ge(S.kload, 128)
    v.tensor_scalar(cur, T.ks[:, :], lowF, sgnF, A.is_ge, A.mult).then_inc(S.s_e, 1)

    te.wait_ge(S.s_w, 2)
    te.wait_ge(S.s_e0, 2)
    te.wait_ge(S.s_e, 1)
    te.matmul(T.dps[:, 0:16], T.wc[:, :], cur, True, False)
    te.matmul(T.dps[:, 0:16], T.wp[:, :], prev, False, True).then_inc(S.s_mm1, 1)
    te.wait_ge(S.s_j, 2)
    te.matmul(T.eps[:, 0:16], T.j0[:, :], cur, True, False)
    te.matmul(T.eps[:, 0:16], T.j16[:, :], cur, False, True).then_inc(S.s_eps, 1)
    te.wait_ge(S.s_w3, 2)
    te.matmul(T.sps[:, 0:16], T.w48[:, :], cur, True, False)

    v.wait_ge(S.s_e0, 2)
    v.wait_ge(S.s_mm1, 1)
    v.tensor_tensor_scan(T.oo[:, :], T.dps[:, 0:16], T.zz[:, :], 0.0, A.add, A.add).then_inc(S.s_o, 1)
    v.wait_ge(S.s_o, 1)
    v.wait_ge(S.s_eps, 1)
    v.tensor_tensor(T.vb[:, :], T.oo[:, :], T.eps[:, 0:16], A.mult).then_inc(S.s_v, 1)
    te.wait_ge(S.s_v, 1)
    te.matmul(T.sps[:, 0:16], T.w3[:, :], T.vb[:, :], False, True).then_inc(S.s_mm2, 1)
    v.wait_ge(S.s_mm2, 1)
    v.tensor_scalar(T.off[:, :], T.sps[:, 0:16], -48.0, None, A.add).then_inc(S.s_off, 1)

    v.wait_ge(S.s_off, 1)
    v.wait_ge(S.s_p, W // 128)
    v.wait_ge(S.xload, 16)
    v.tensor_copy(T.pk[:, 0:W].indirect(T.off[:, 0:16]), T.xs[:, 0:TC]).then_inc(S.s_sc, 1)

    v.wait_ge(S.s_p2, 1)
    v.wait_ge(S.x2_in, len(all_eng))
    v.wait_ge(S.off2_in, len(chip_eng))
    v.tensor_copy(T.pk2[:, 0:W].indirect(T.off2[:, 0:16]), T.x2[:, 0:TC]).then_inc(S.s_sc2, 1)

    g.wait_ge(S.s_sc, 1)
    fr = sorted(T.rank_of(d) for d in far)
    rid, pid = topo.addr(relay, core)
    g.remote_dma(T.hop[:, :], blk(T.pk, fr[0], len(fr)), S.hop_in, S.sent, pid, rid, _bits(off_eng))
    sent += len(off_eng)
    per = len(off_eng) // len(order)
    trs = []
    for i, d in enumerate(order):
        rid, pid = topo.addr(d, core)
        trs.append(RemoteDMATransfer(dst_ids=[DstId(rid=rid, pnc=pid)], dma_engine_mask=_bits(off_eng[i::len(order)]),
                                     remote_sem=S.near_in, src=blk(T.pk, T.rank_of(d)), dst=blk(T.land, rank)))
        sent += per
    g.remote_dma_fused(trs, local_sem=S.sent)
    g.remote_dma(T.off2[:, :], T.off[:, :], S.off2_in, S.sent, mpid, mrid, _bits(chip_eng))
    sent += len(chip_eng)

    g.wait_ge(S.hop_in, len(off_eng))
    dsts = sorted(_far(feeder, cores, topo), key=T.rank_of)
    half = len(off_eng) // len(dsts)
    trs = []
    for i, d in enumerate(dsts):
        rid, pid = topo.addr(d, core)
        trs.append(RemoteDMATransfer(dst_ids=[DstId(rid=rid, pnc=pid)], dma_engine_mask=_bits(off_eng[i::len(dsts)]),
                                     remote_sem=S.far_in, src=blk(T.hop, i), dst=blk(T.land, T.rank_of(feeder))))
        sent += half
    g.remote_dma_fused(trs, local_sem=S.sent)

    stored = 0
    g.scalar.wait_ge(S.s_sc, 1)
    g.scalar.dma_start(blk(T.y, rank), blk(T.pk, rank)).then_inc(S.stored, 16)
    stored += 16
    g.scalar.wait_ge(S.near_in, per * len(order))
    for r0, n in _runs(T.rank_of(d) for d in away):
        g.scalar.dma_start(blk(T.y, r0, n), blk(T.land, r0, n)).then_inc(S.stored, 16)
        stored += 16
    g.sync.wait_ge(S.s_sc2, 1)
    g.sync.dma_start(blk(T.y, T.rank_of(mate)), blk(T.pk2, rank)).then_inc(S.stored, 16)
    stored += 16
    g.sync.wait_ge(S.far_in, half * len(far))
    for r0, n in _runs(fr):
        g.sync.dma_start(blk(T.y, r0, n), blk(T.land, r0, n)).then_inc(S.stored, 16)
        stored += 16
    g.wait_ge(S.sent, sent)
    g.wait_ge(S.stored, stored)
